import numpy as np
import ml_dtypes


def mxq(x, axis, fmt="e4m3"):
    dtype, down = {"e4m3": (ml_dtypes.float8_e4m3fn, 7), "e5m2": (ml_dtypes.float8_e5m2, 14)}[fmt]
    v = np.moveaxis(np.asarray(x, np.float32).astype(ml_dtypes.bfloat16).astype(np.float64), axis, -1)
    blocks = v.reshape(v.shape[:-1] + (-1, 32))
    amax = np.abs(blocks).max(-1, keepdims=True)
    byte = np.maximum(np.where(amax > 0, np.frexp(amax)[1] - 1 + 127, 0) - down, 1)
    scale = np.exp2(byte - 127.0)
    codes = (blocks / scale).astype(np.float32).astype(dtype).astype(np.float64)
    return np.moveaxis((codes * scale).reshape(v.shape), -1, axis)


WIDE = False


def mx_kscale(k):
    if not WIDE:
        return np.ones(k)
    levels = np.array([10, -10, 5, -5, 0])
    if k % 512:
        return np.exp2(np.random.permutation(np.resize(levels, k // 32))).repeat(32)
    a = np.empty((k // 512, 16))
    for p in range(k // 512):
        a[p, :8] = np.random.permutation(np.resize(levels, 8))
        for g in range(8):
            far = levels[np.abs(levels - a[p, g]) >= 10]
            a[p, g + 8] = far[np.random.randint(len(far))]
    return np.exp2(a.ravel()).repeat(32)


def f64(x):
    return np.asarray(x).astype(np.float64)


def striped(idx):
    return np.tile(idx.reshape(-1, 16).T, (8, 1)).astype(np.uint16)


def unstriped(offs):
    return offs[:16].T.reshape(-1).astype(np.int64)


def striped8(idx):
    return np.concatenate([x.reshape(-1, 16).T for x in idx]).astype(np.uint16)


def runs(offs, k):
    lists = np.stack([offs[16 * r : 16 * r + 16].T.reshape(-1) for r in range(8)]).astype(np.int64)
    return lists[np.arange(k) % 512 // 64]


def pack_weight(w):
    k, n = w.shape
    w = f64(np.asarray(w, np.float32).astype(ml_dtypes.bfloat16)).reshape(k // 32, 32, n)
    amax = np.abs(w).max(1)
    byte = np.clip(np.where(amax > 0, np.frexp(amax)[1] - 1 + 127 - 7, 1), 1, 254)
    scaled = (w * np.exp2(127.0 - byte)[:, None, :]).reshape(k, n).astype(np.float32)
    words = np.ascontiguousarray(scaled.reshape(k // 512, 128, 4, n).transpose(0, 1, 3, 2)).astype(ml_dtypes.float8_e4m3fn).view(np.uint8)
    return words, np.ascontiguousarray(byte.astype(np.uint8).reshape(k // 512, 16, n))


def unpack_weight(words, scales):
    g, p, n, _ = words.shape
    vals = np.ascontiguousarray(words).view(ml_dtypes.float8_e4m3fn).astype(np.float64) * np.repeat(np.exp2(scales.astype(np.float64) - 127.0), 8, axis=1)[..., None]
    return vals.transpose(0, 1, 3, 2).reshape(g * 512, n)


K, T, S, H, C = 512, 2048, 512, 512, 512


def setup_inputs():
    n = np.random.standard_normal
    s = mx_kscale(K)[:, None]
    packed_xT = pack_weight(n((K, T)) * s)
    return {
        "x_words": packed_xT[0],
        "x_scales": packed_xT[1],
        "w1": (n((K, H)) / np.sqrt(K) / s).astype(np.float32),
        "w2": (n((K, H)) / np.sqrt(K) / s).astype(np.float32),
        "gs": (np.random.uniform(0.5, 1.5, (K, 1)) / s).astype(np.float32),
        "offs": striped(np.random.permutation(T)[:S]),
        "two": striped(np.random.permutation(T)[:S]),
        "n1": striped8(np.stack([np.random.permutation(S) for _ in range(8)])),
        "n2": striped8(np.stack([np.random.permutation(S) for _ in range(8)])),
        "n3": striped8(np.stack([np.random.permutation(S) for _ in range(8)])),
        "cand": striped(np.random.permutation(T)[:C]),
        "n4": striped8(np.stack([np.random.permutation(S) for _ in range(8)])),
        "n5": striped8(np.stack([np.random.permutation(S) for _ in range(8)])),
        "n6": striped8(np.stack([np.random.permutation(S) for _ in range(8)])),
    }


def reference(x_words, x_scales, w1, w2, gs, offs, two, n1, n2, n3, cand, n4, n5, n6):
    x_cand = unpack_weight(x_words, x_scales)[:, unstriped(cand)]
    x_two = unpack_weight(x_words, x_scales)[:, unstriped(two)]
    d = mxq(f64(w2), 0, "e4m3").T @ x_two
    xq = unpack_weight(x_words, x_scales)[:, unstriped(offs)]
    y = mxq(f64(w1), 0, "e4m3").T @ xq
    z = f64(gs) * (d * (y[np.arange(H)[:, None], runs(n1, H)] - y) + 0.5 * ((d[np.arange(H)[:, None], runs(n3, H)]) * (y[np.arange(H)[:, None], runs(n2, H)] - y)))
    s = 0.0625 * ((x_cand.T @ mxq(z, 0, "e4m3")))
    ex = np.exp(0.5 * s)
    return np.log((ex + ex[np.arange(C)[:, None], runs(n4, C)]) / (ex[np.arange(C)[:, None], runs(n5, C)] + ex[np.arange(C)[:, None], runs(n6, C)]))

@@ -1,0 +1,243 @@
+from contextlib import ExitStack
+
+import concourse.mybir as mybir
+from concourse.masks import make_identity
+
+FLOPS = 3 * 2 * 512 * 512 * 512
+
+F32 = mybir.dt.float32
+BF16 = mybir.dt.bfloat16
+I32 = mybir.dt.int32
+U32 = mybir.dt.uint32
+U16 = mybir.dt.uint16
+U8 = mybir.dt.uint8
+FP8X4 = mybir.dt.float8_e4m3fn_x4
+ALU = mybir.AluOpType
+ACT = mybir.ActivationFunctionType
+
+P = 128
+T = 2048
+S = 512
+NT = 4
+CHUNKS = ((0, 256), (256, 384), (384, 512))
+SCALAR_TILES = (1, 2, 3)
+
+
+def tile_picked_twcflowbodds_none_p_kernel(
+    tc, x_words, x_scales, w1, w2, gs, offs, two, n1, n2, n3, cand, n4, n5, n6, out
+):
+    nc = tc.nc
+    with ExitStack() as ctx:
+        keep = ctx.enter_context(tc.tile_pool(name="keep", bufs=1))
+        work = ctx.enter_context(tc.tile_pool(name="work", bufs=1))
+        psum = ctx.enter_context(tc.psum_pool(name="psum", bufs=1))
+
+        def load_list(src, name):
+            tl = keep.tile([P, S // 16], U16, name=name)
+            nc.sync.dma_start(tl[:], src)
+            return tl
+
+        warm = work.tile([P, 2], F32, name="warm")
+        nc.vector.memset(warm[:, 0:1], 0.0)
+        nc.scalar.activation(warm[:, 1:2], warm[:, 0:1], ACT.Exp)
+
+        xs = work.tile([P, T], U8, name="xs")
+        nc.vector.memset(xs[:].bitcast(I32), 0)
+        l_offs = load_list(offs, "l_offs")
+        for q in range(4):
+            nc.sync.dma_start(xs[32 * q : 32 * q + 4, :].bitcast(I32), x_scales[0, 4 * q : 4 * q + 4, :].bitcast(I32))
+        l_two = load_list(two, "l_two")
+        w1raw = work.tile([P, 4, S], F32, name="w1raw")
+        nc.sync.dma_start(w1raw[:], w1.rearrange("(p j) c -> p j c", j=4))
+        xw = work.tile([P, T], I32, name="xw")
+        nc.sync.dma_start(xw[:], x_words[0].rearrange("p n t -> p (n t)").bitcast(I32))
+        l_cand = load_list(cand, "l_cand")
+        w2raw = work.tile([P, 4, S], F32, name="w2raw")
+        nc.sync.dma_start(w2raw[:], w2.rearrange("(p j) c -> p j c", j=4))
+        l_n1 = load_list(n1, "l_n1")
+        l_n2 = load_list(n2, "l_n2")
+        gst = work.tile([P, NT], F32, name="gst")
+        nc.sync.dma_start(gst[:], gs.rearrange("(p t) o -> p (t o)", t=NT))
+        l_n3 = load_list(n3, "l_n3")
+        l_n5 = load_list(n5, "l_n5")
+        l_n6 = load_list(n6, "l_n6")
+        l_n4 = load_list(n4, "l_n4")
+
+        win = [work.tile([P, 2 * S], F32, name="win%d" % t) for t in range(NT)]
+        for t in range(NT):
+            nc.gpsimd.memset(win[t][:, S:], 0.0)
+        ident = work.tile([P, P], F32, name="ident")
+        make_identity(nc, ident[:])
+        hgs = work.tile([P, NT], F32, name="hgs")
+        nc.gpsimd.tensor_scalar(hgs[:], gst[:], 0.5, 0.0, ALU.mult, ALU.add)
+        uwin = {}
+        for t in SCALAR_TILES:
+            uwin[t] = work.tile([P, 2 * S], F32, name="uwin%d" % t, tag="uwin%d" % t)
+            nc.gpsimd.memset(uwin[t][:, S:], 0.0)
+
+        def gather_scales(lst, name):
+            g = work.tile([P, S], U8, name=name, align_bytes=64)
+            nc.vector.tensor_copy(g[:], xs[:].indirect(lst[:]))
+            return g
+
+        def gather_words(lst, name, tag, bufs):
+            g = work.tile([P, S], U32, name=name, tag=tag, bufs=bufs, align_bytes=64)
+            nc.vector.tensor_copy(g[:], xw[:].bitcast(U32).indirect(lst[:]))
+            return g
+
+        def cast_pair(raw, u, name):
+            wb = work.tile([P, 2, P, 4], BF16, name=name, align_bytes=64)
+            nc.scalar.copy(
+                wb[:].rearrange("p e m j -> p m j e"),
+                raw[:].rearrange("p j (m t) -> p m j t", t=NT)[:, :, :, 2 * u : 2 * u + 2],
+            )
+            return wb
+
+        def quant_pair(wb, name):
+            codes = work.tile([P, 2 * P], U32, name=name + "c", align_bytes=64)
+            sc = work.tile([P, 2 * P], U8, name=name + "s", align_bytes=64)
+            nc.vector.quantize_mx(codes[:].bitcast(FP8X4), sc[:], wb[:].rearrange("p e m j -> p (e m j)"))
+            return codes, sc
+
+        def product(lc, ls, col, rc, rs):
+            acc = psum.tile([P, S], F32, name="acc", tag="acc", bufs=4)
+            nc.tensor.matmul_mx(
+                acc[:], lhsT=lc[:, col : col + P].bitcast(FP8X4), lhsT_scale=ls[:, col : col + P],
+                rhs=rc[:].bitcast(FP8X4), rhs_scale=rs[:], start=True, stop=True,
+            )
+            return acc
+
+        s_offs = gather_scales(l_offs, "s_offs")
+        s_two = gather_scales(l_two, "s_two")
+        w1b = [cast_pair(w1raw, u, "w1b%d" % u) for u in range(2)]
+        s_cand = gather_scales(l_cand, "s_cand")
+        w1q = [quant_pair(w1b[u], "w1q%d" % u) for u in range(2)]
+        g_offs = gather_words(l_offs, "g_offs", "g_offs", 1)
+        g_two = gather_words(l_two, "g_two", "g_two", 1)
+        s_candd = work.tile([P, S], U8, name="s_candd", align_bytes=64)
+        nc.vector.tensor_copy(s_candd[:].rearrange("p (t m) -> p t m", t=NT), s_cand[:].rearrange("p (m t) -> p t m", t=NT))
+
+        yp = [work.tile([P, S], F32, name="yp%d" % t) for t in range(NT)]
+        da = [work.tile([P, S], F32, name="da%d" % t) for t in range(NT)]
+        db = [work.tile([P, S], F32, name="db%d" % t, tag="db", bufs=NT, align_bytes=64) for t in range(NT)]
+        dwin = [work.tile([P, S], F32, name="dwin%d" % t) for t in range(NT)]
+        w2q = []
+
+        def y_tile(t):
+            acc = product(w1q[t // 2][0], w1q[t // 2][1], (t % 2) * P, g_offs, s_offs)
+            nc.scalar.copy(win[t][:, :S], acc[:])
+            nc.scalar.copy(yp[t][:], acc[:])
+
+        def diffs(t):
+            nc.vector.tensor_tensor(da[t][:], win[t][:].indirect(l_n1[:]), yp[t][:], ALU.subtract)
+            nc.vector.tensor_tensor(db[t][:], win[t][:].indirect(l_n2[:]), yp[t][:], ALU.subtract)
+
+        def d_tile(t):
+            acc = product(w2q[t // 2][0], w2q[t // 2][1], (t % 2) * P, g_two, s_two)
+            nc.scalar.activation(dwin[t][:], acc[:], ACT.Copy, scale=hgs[:, t : t + 1])
+
+        y_tile(0)
+        y_tile(1)
+        diffs(0)
+        w2b0 = cast_pair(w2raw, 0, "w2b0")
+        y_tile(2)
+        diffs(1)
+        w2q.append(quant_pair(w2b0, "w2q0"))
+        w2b1 = cast_pair(w2raw, 1, "w2b1")
+        y_tile(3)
+        diffs(2)
+        w2q.append(quant_pair(w2b1, "w2q1"))
+        for t in range(NT):
+            d_tile(t)
+        diffs(3)
+
+        te = [work.tile([P, S], F32, name="te%d" % t) for t in range(NT)]
+        tc3 = [work.tile([P, S], F32, name="tc%d" % t) for t in range(NT)]
+        zq = work.tile([P, S], U32, name="zq", align_bytes=64)
+        zs = work.tile([P, S], U8, name="zs", align_bytes=64)
+        zb = {}
+
+        def first_terms(lo, hi):
+            for t in range(NT):
+                nc.vector.scalar_tensor_tensor(te[t][:, lo:hi], dwin[t][:, lo:hi], 2.0, da[t][:, lo:hi], ALU.mult, ALU.mult)
+
+        def second_terms(lo, hi):
+            for t in range(NT):
+                nc.vector.tensor_tensor(tc3[t][:, lo:hi], dwin[t][:].indirect(l_n3[:, lo // 16 : hi // 16]), db[t][:, lo:hi], ALU.mult)
+
+        def turn(lo, hi):
+            zb[lo] = work.tile([P, hi - lo, 2], F32, name="zb%d" % lo, align_bytes=64)
+            for j0 in range(lo, hi, P):
+                zt = psum.tile([P, NT, P], F32, name="zt", tag="zt", bufs=2)
+                for t in range(NT):
+                    nc.tensor.matmul(zt[:, t, :], te[t][:, j0 : j0 + P], ident[:], start=True, stop=False, is_transpose=True)
+                    nc.tensor.matmul(zt[:, t, :], tc3[t][:, j0 : j0 + P], ident[:], start=False, stop=True, is_transpose=True)
+                ztb = work.tile([P, 2, P, 2], BF16, name="ztb", tag="ztb", bufs=2)
+                nc.scalar.copy(ztb[:], zt[:].rearrange("j (u e) p -> j u p e", e=2))
+                words = ztb[:].rearrange("j u p e -> j (u p e)").bitcast(F32)
+                zw = psum.tile([P, 2, P], F32, name="zw", tag="zw", bufs=2)
+                for u in range(2):
+                    nc.tensor.transpose(zw[:, u, :], words[:, u * P : (u + 1) * P], ident[:])
+                nc.scalar.copy(zb[lo][:, j0 - lo : j0 - lo + P, :], zw[:].rearrange("p u j -> p j u"))
+
+        def quant_z(lo, hi):
+            nc.vector.quantize_mx(zq[:, lo:hi].bitcast(FP8X4), zs[:, lo:hi], zb[lo][:].rearrange("p j u -> p (j u)").bitcast(BF16))
+
+        first_terms(0, 256)
+        second_terms(0, 256)
+        turn(0, 256)
+        first_terms(256, 512)
+        second_terms(256, 384)
+        turn(256, 384)
+        quant_z(0, 256)
+        second_terms(384, 512)
+        turn(384, 512)
+        g_cand = gather_words(l_cand, "g_cand", "db", NT)
+        quant_z(256, 384)
+        g_candd = work.tile([P, S], U32, name="g_candd", align_bytes=64)
+        nc.vector.tensor_copy(
+            g_candd[:].rearrange("p (t c i) -> p c t i", t=NT, i=4),
+            g_cand[:].rearrange("p (c i t) -> p c t i", t=NT, i=4),
+        )
+        quant_z(384, 512)
+
+        exp_plain = [work.tile([P, S], F32, name="exp%d" % t) for t in range(NT)]
+        e5 = [work.tile([P, S], F32, name="e5_%d" % t) for t in range(NT)]
+        num = [work.tile([P, S], F32, name="num%d" % t) for t in range(NT)]
+        den = [work.tile([P, S], F32, name="den%d" % t) for t in range(NT)]
+        accs = [product(g_candd, s_candd, t * P, zq, zs) for t in range(NT)]
+
+        def ex_tile(t):
+            nc.scalar.activation(win[t][:, :S], accs[t][:], ACT.Exp, scale=0.03125)
+            nc.sync.dma_start(exp_plain[t][:], win[t][:, :S])
+
+        def u_tile(t):
+            nc.scalar.activation(uwin[t][:, :S], accs[t][:], ACT.Copy, scale=0.03125)
+
+        def e5_tile(t):
+            nc.scalar.activation(e5[t][:], uwin[t][:].indirect(l_n5[:]), ACT.Exp)
+
+        ex_tile(0)
+        nc.vector.tensor_copy(e5[0][:], win[0][:].indirect(l_n5[:]))
+        u_tile(1)
+        ex_tile(1)
+        e5_tile(1)
+        u_tile(2)
+        ex_tile(2)
+        u_tile(3)
+        e5_tile(2)
+        ex_tile(3)
+        e5_tile(3)
+        for t in range(NT):
+            nc.vector.tensor_tensor(den[t][:], win[t][:].indirect(l_n6[:]), e5[t][:], ALU.add)
+            nc.vector.tensor_tensor(num[t][:], win[t][:].indirect(l_n4[:]), exp_plain[t][:], ALU.add)
+        out_rows = out.rearrange("(p t) n -> p t n", t=NT)
+        logs = work.tile([P, 2 * NT * S], F32, name="logs", tag="uwin3")
+        for t in range(NT):
+            lden = logs[:, 2 * t * S : (2 * t + 1) * S]
+            lnum = logs[:, (2 * t + 1) * S : (2 * t + 2) * S]
+            nc.scalar.activation(lden, den[t][:], ACT.Ln)
+            nc.scalar.activation(lnum, num[t][:], ACT.Ln)
+            res = work.tile([P, S], F32, name="res%d" % t)
+            nc.vector.tensor_tensor(res[:], lnum, lden, ALU.subtract)
+            nc.sync.dma_start(out_rows[:, t, :], res[:])

@@ -18,8 +18,12 @@ ACT = mybir.ActivationFunctionType
 P = 128
 T = 2048
 S = 512
-NT = 4
-CHUNKS = ((0, 256), (256, 384), (384, 512))
+HALF = S // 2
+TILES = 4
+BLOCKS = S // P
+LAST = S - P
+STRIPE = 16
+EXP_SCALE = 0.5 * 0.0625
 SCALAR_TILES = (1, 2, 3)
 
 
@@ -28,216 +32,278 @@ def tile_picked_twcflowbodds_none_p_kernel(
 ):
     nc = tc.nc
     with ExitStack() as ctx:
-        keep = ctx.enter_context(tc.tile_pool(name="keep", bufs=1))
+        lists = ctx.enter_context(tc.tile_pool(name="lists", bufs=1))
         work = ctx.enter_context(tc.tile_pool(name="work", bufs=1))
         psum = ctx.enter_context(tc.psum_pool(name="psum", bufs=1))
 
         def load_list(src, name):
-            tl = keep.tile([P, S // 16], U16, name=name)
-            nc.sync.dma_start(tl[:], src)
-            return tl
+            offsets = lists.tile([P, S // STRIPE], U16, name=name)
+            nc.sync.dma_start(offsets[:], src)
+            return offsets
 
-        warm = work.tile([P, 2], F32, name="warm")
-        nc.vector.memset(warm[:, 0:1], 0.0)
-        nc.scalar.activation(warm[:, 1:2], warm[:, 0:1], ACT.Exp)
-
-        xs = work.tile([P, T], U8, name="xs")
-        nc.vector.memset(xs[:].bitcast(I32), 0)
+        scale_table = work.tile([P, T], U8, name="scale_table")
+        nc.gpsimd.memset(scale_table[:].bitcast(I32), 0)
         l_offs = load_list(offs, "l_offs")
-        for q in range(4):
-            nc.sync.dma_start(xs[32 * q : 32 * q + 4, :].bitcast(I32), x_scales[0, 4 * q : 4 * q + 4, :].bitcast(I32))
         l_two = load_list(two, "l_two")
-        w1raw = work.tile([P, 4, S], F32, name="w1raw")
-        nc.sync.dma_start(w1raw[:], w1.rearrange("(p j) c -> p j c", j=4))
-        xw = work.tile([P, T], I32, name="xw")
-        nc.sync.dma_start(xw[:], x_words[0].rearrange("p n t -> p (n t)").bitcast(I32))
+        w1_raw = work.tile([P, TILES, S], F32, name="w1_raw")
+        w1_rows = w1.rearrange("(p j) c -> p j c", j=TILES)
+        nc.sync.dma_start(w1_raw[:, 0, :], w1_rows[:, 0, :])
+        for quad in range(4):
+            nc.sync.dma_start(
+                scale_table[32 * quad : 32 * quad + 4, :].bitcast(I32),
+                x_scales[0, 4 * quad : 4 * quad + 4, :].bitcast(I32),
+            )
+        nc.sync.dma_start(w1_raw[:, 1:, :], w1_rows[:, 1:, :])
         l_cand = load_list(cand, "l_cand")
-        w2raw = work.tile([P, 4, S], F32, name="w2raw")
-        nc.sync.dma_start(w2raw[:], w2.rearrange("(p j) c -> p j c", j=4))
+        word_table = work.tile([P, T], I32, name="word_table")
+        nc.sync.dma_start(word_table[:], x_words[0].rearrange("p n t -> p (n t)").bitcast(I32))
         l_n1 = load_list(n1, "l_n1")
         l_n2 = load_list(n2, "l_n2")
-        gst = work.tile([P, NT], F32, name="gst")
-        nc.sync.dma_start(gst[:], gs.rearrange("(p t) o -> p (t o)", t=NT))
+        w2_raw = work.tile([P, TILES, S], F32, name="w2_raw")
+        nc.sync.dma_start(w2_raw[:], w2.rearrange("(p j) c -> p j c", j=TILES))
+        gains = work.tile([P, TILES], F32, name="gains")
+        nc.sync.dma_start(gains[:], gs.rearrange("(p t) o -> p (t o)", t=TILES))
         l_n3 = load_list(n3, "l_n3")
         l_n5 = load_list(n5, "l_n5")
         l_n6 = load_list(n6, "l_n6")
         l_n4 = load_list(n4, "l_n4")
 
-        win = [work.tile([P, 2 * S], F32, name="win%d" % t) for t in range(NT)]
-        for t in range(NT):
-            nc.gpsimd.memset(win[t][:, S:], 0.0)
+        rows = [work.tile([P, 2 * S], F32, name="rows%d" % t) for t in range(TILES)]
+        nc.vector.memset(rows[0][:, S : S + HALF], 0.0)
+        nc.scalar.copy(rows[0][:, S + HALF :], rows[0][:, S : S + HALF])
         ident = work.tile([P, P], F32, name="ident")
         make_identity(nc, ident[:])
-        hgs = work.tile([P, NT], F32, name="hgs")
-        nc.gpsimd.tensor_scalar(hgs[:], gst[:], 0.5, 0.0, ALU.mult, ALU.add)
-        uwin = {}
-        for t in SCALAR_TILES:
-            uwin[t] = work.tile([P, 2 * S], F32, name="uwin%d" % t, tag="uwin%d" % t)
-            nc.gpsimd.memset(uwin[t][:, S:], 0.0)
+        args = {t: work.tile([P, 2 * S], F32, name="args%d" % t, tag="args%d" % t) for t in SCALAR_TILES}
 
-        def gather_scales(lst, name):
-            g = work.tile([P, S], U8, name=name, align_bytes=64)
-            nc.vector.tensor_copy(g[:], xs[:].indirect(lst[:]))
-            return g
+        def gather_scales(offsets, name):
+            picked = work.tile([P, S], U8, name=name, align_bytes=64)
+            nc.vector.tensor_copy(picked[:], scale_table[:].indirect(offsets[:]))
+            return picked
 
-        def gather_words(lst, name, tag, bufs):
-            g = work.tile([P, S], U32, name=name, tag=tag, bufs=bufs, align_bytes=64)
-            nc.vector.tensor_copy(g[:], xw[:].bitcast(U32).indirect(lst[:]))
-            return g
+        def gather_words(picked, offsets, lo, hi):
+            entries = offsets[:, lo // STRIPE : hi // STRIPE]
+            nc.vector.tensor_copy(picked[:, lo:hi], word_table[:].bitcast(U32).indirect(entries))
 
         def cast_pair(raw, u, name):
-            wb = work.tile([P, 2, P, 4], BF16, name=name, align_bytes=64)
+            rounded = work.tile([P, 2, P, TILES], BF16, name=name, align_bytes=64)
             nc.scalar.copy(
-                wb[:].rearrange("p e m j -> p m j e"),
-                raw[:].rearrange("p j (m t) -> p m j t", t=NT)[:, :, :, 2 * u : 2 * u + 2],
+                rounded[:].rearrange("p e m j -> p m j e"),
+                raw[:].rearrange("p j (m t) -> p m j t", t=TILES)[:, :, :, 2 * u : 2 * u + 2],
             )
-            return wb
+            return rounded
 
-        def quant_pair(wb, name):
-            codes = work.tile([P, 2 * P], U32, name=name + "c", align_bytes=64)
-            sc = work.tile([P, 2 * P], U8, name=name + "s", align_bytes=64)
-            nc.vector.quantize_mx(codes[:].bitcast(FP8X4), sc[:], wb[:].rearrange("p e m j -> p (e m j)"))
-            return codes, sc
+        def quantise_weights(rounded, e0, e1, name, tag):
+            words = work.tile([P, (e1 - e0) * P], U32, name=name + "_words", tag=tag, align_bytes=64)
+            scales = work.tile([P, (e1 - e0) * P], U8, name=name + "_scales", align_bytes=64)
+            values = rounded[:, e0:e1, :, :].rearrange("p e m j -> p (e m j)")
+            nc.vector.quantize_mx(words[:].bitcast(FP8X4), scales[:], values)
+            return [(words[:, e * P : (e + 1) * P], scales[:, e * P : (e + 1) * P]) for e in range(e1 - e0)]
 
-        def product(lc, ls, col, rc, rs):
-            acc = psum.tile([P, S], F32, name="acc", tag="acc", bufs=4)
+        def bank(tag, width):
+            return psum.tile([P, width], F32, name=tag, tag=tag, bufs=TILES if tag == "ring" else 1)
+
+        def mx_pass(dst, stationary, moving, lo, hi):
             nc.tensor.matmul_mx(
-                acc[:], lhsT=lc[:, col : col + P].bitcast(FP8X4), lhsT_scale=ls[:, col : col + P],
-                rhs=rc[:].bitcast(FP8X4), rhs_scale=rs[:], start=True, stop=True,
+                dst,
+                lhsT=stationary[0].bitcast(FP8X4),
+                lhsT_scale=stationary[1],
+                rhs=moving[0][:, lo:hi].bitcast(FP8X4),
+                rhs_scale=moving[1][:, lo:hi],
+                start=True,
+                stop=True,
             )
+
+        def product(stationary, moving, tag, lo=0, hi=S):
+            acc = bank(tag, hi - lo)
+            mx_pass(acc[:], stationary, moving, lo, hi)
             return acc
 
-        s_offs = gather_scales(l_offs, "s_offs")
-        s_two = gather_scales(l_two, "s_two")
-        w1b = [cast_pair(w1raw, u, "w1b%d" % u) for u in range(2)]
-        s_cand = gather_scales(l_cand, "s_cand")
-        w1q = [quant_pair(w1b[u], "w1q%d" % u) for u in range(2)]
-        g_offs = gather_words(l_offs, "g_offs", "g_offs", 1)
-        g_two = gather_words(l_two, "g_two", "g_two", 1)
-        s_candd = work.tile([P, S], U8, name="s_candd", align_bytes=64)
-        nc.vector.tensor_copy(s_candd[:].rearrange("p (t m) -> p t m", t=NT), s_cand[:].rearrange("p (m t) -> p t m", t=NT))
+        scales_offs = gather_scales(l_offs, "scales_offs")
+        scales_two = gather_scales(l_two, "scales_two")
+        w1_rounded = [cast_pair(w1_raw, u, "w1_rounded%d" % u) for u in range(2)]
+        w1q = quantise_weights(w1_rounded[0], 0, 1, "w1q0", "w1q0")
+        w1q = w1q + quantise_weights(w1_rounded[0], 1, 2, "w1q1", "w1q1")
+        scales_cand = gather_scales(l_cand, "scales_cand")
+        words_offs = work.tile([P, S], U32, name="words_offs", align_bytes=64)
+        for lo in (0, HALF):
+            gather_words(words_offs, l_offs, lo, lo + HALF)
+        words_two = work.tile([P, S], U32, name="words_two", align_bytes=64)
+        gather_words(words_two, l_two, 0, S)
+        x_offs = (words_offs, scales_offs)
+        x_two = (words_two, scales_two)
 
-        yp = [work.tile([P, S], F32, name="yp%d" % t) for t in range(NT)]
-        da = [work.tile([P, S], F32, name="da%d" % t) for t in range(NT)]
-        db = [work.tile([P, S], F32, name="db%d" % t, tag="db", bufs=NT, align_bytes=64) for t in range(NT)]
-        dwin = [work.tile([P, S], F32, name="dwin%d" % t) for t in range(NT)]
+        y_plain = [rows[t + 1][:, S:] for t in range(TILES - 1)] + [work.tile([P, S], F32, name="y_plain3")[:]]
+        diff1 = [args[t][:, S:] if t in args else work.tile([P, S], F32, name="diff1_%d" % t)[:] for t in range(TILES)]
+        diff2 = [
+            work.tile([P, S], F32, name="diff2_%d" % t, tag="diff2", bufs=TILES, align_bytes=64) for t in range(TILES)
+        ]
+        gained_d = [work.tile([P, S], F32, name="gained_d%d" % t) for t in range(TILES)]
         w2q = []
 
         def y_tile(t):
-            acc = product(w1q[t // 2][0], w1q[t // 2][1], (t % 2) * P, g_offs, s_offs)
-            nc.scalar.copy(win[t][:, :S], acc[:])
-            nc.scalar.copy(yp[t][:], acc[:])
+            for lo, hi in ((0, HALF), (HALF, S)) if t == 0 else ((0, S),):
+                acc = product(w1q[t], x_offs, "ring", lo, hi)
+                nc.scalar.copy(rows[t][:, lo:hi], acc[:])
+                nc.scalar.copy(y_plain[t][:, lo:hi], acc[:])
 
-        def diffs(t):
-            nc.vector.tensor_tensor(da[t][:], win[t][:].indirect(l_n1[:]), yp[t][:], ALU.subtract)
-            nc.vector.tensor_tensor(db[t][:], win[t][:].indirect(l_n2[:]), yp[t][:], ALU.subtract)
+        def differences(t):
+            nc.vector.tensor_tensor(diff1[t], rows[t][:].indirect(l_n1[:]), y_plain[t], ALU.subtract)
+            nc.vector.tensor_tensor(diff2[t][:], rows[t][:].indirect(l_n2[:]), y_plain[t], ALU.subtract)
 
         def d_tile(t):
-            acc = product(w2q[t // 2][0], w2q[t // 2][1], (t % 2) * P, g_two, s_two)
-            nc.scalar.activation(dwin[t][:], acc[:], ACT.Copy, scale=hgs[:, t : t + 1])
+            acc = product(w2q[t], x_two, "side%d" % (t % 2))
+            nc.scalar.activation(gained_d[t][:], acc[:], ACT.Copy, scale=gains[:, t : t + 1])
 
         y_tile(0)
+        w1q.extend(quantise_weights(w1_rounded[1], 0, 2, "w1q2", "w1q0"))
         y_tile(1)
-        diffs(0)
-        w2b0 = cast_pair(w2raw, 0, "w2b0")
+        differences(0)
+        w2_rounded0 = cast_pair(w2_raw, 0, "w2_rounded0")
         y_tile(2)
-        diffs(1)
-        w2q.append(quant_pair(w2b0, "w2q0"))
-        w2b1 = cast_pair(w2raw, 1, "w2b1")
+        differences(1)
+        w2q.extend(quantise_weights(w2_rounded0, 0, 2, "w2q0", "w2q0"))
+        w2_rounded1 = cast_pair(w2_raw, 1, "w2_rounded1")
         y_tile(3)
-        diffs(2)
-        w2q.append(quant_pair(w2b1, "w2q1"))
-        for t in range(NT):
+        differences(2)
+        w2q.extend(quantise_weights(w2_rounded1, 0, 2, "w2q2", "w2q2"))
+        for t in range(TILES):
             d_tile(t)
-        diffs(3)
+        differences(3)
 
-        te = [work.tile([P, S], F32, name="te%d" % t) for t in range(NT)]
-        tc3 = [work.tile([P, S], F32, name="tc%d" % t) for t in range(NT)]
-        zq = work.tile([P, S], U32, name="zq", align_bytes=64)
-        zs = work.tile([P, S], U8, name="zs", align_bytes=64)
-        zb = {}
+        term1 = [work.tile([P, S], F32, name="term1_%d" % t) for t in range(TILES)]
+        term2 = [work.tile([P, S], F32, name="term2_%d" % t) for t in range(TILES)]
+        z_words = work.tile([P, S], U32, name="z_words", align_bytes=64)
+        z_scales = work.tile([P, S], U8, name="z_scales", align_bytes=64)
+        turned = [bank("ring", S) for b in range(BLOCKS)]
+        turned_pairs = [[turned[b][:, :HALF], turned[b][:, HALF:]] for b in range(BLOCKS - 1)]
+        turned_pairs.append([turned[BLOCKS - 1][:, :HALF], bank("side0", HALF)[:]])
+        z_rounded = {}
 
-        def first_terms(lo, hi):
-            for t in range(NT):
-                nc.vector.scalar_tensor_tensor(te[t][:, lo:hi], dwin[t][:, lo:hi], 2.0, da[t][:, lo:hi], ALU.mult, ALU.mult)
+        def add_turned(term, t, b, start, stop):
+            dst = turned_pairs[b][t // 2][:, (t % 2) * P : (t % 2 + 1) * P]
+            nc.tensor.matmul(dst, term[:, b * P : (b + 1) * P], ident[:], start=start, stop=stop, is_transpose=True)
 
-        def second_terms(lo, hi):
-            for t in range(NT):
-                nc.vector.tensor_tensor(tc3[t][:, lo:hi], dwin[t][:].indirect(l_n3[:, lo // 16 : hi // 16]), db[t][:, lo:hi], ALU.mult)
+        def first_terms():
+            for t in range(TILES):
+                nc.vector.scalar_tensor_tensor(term1[t][:], gained_d[t][:], 2.0, diff1[t], ALU.mult, ALU.mult)
+                for b in range(BLOCKS):
+                    first_in_bank = t == 0 or (t == 2 and b == BLOCKS - 1)
+                    add_turned(term1[t], t, b, first_in_bank, False)
 
-        def turn(lo, hi):
-            zb[lo] = work.tile([P, hi - lo, 2], F32, name="zb%d" % lo, align_bytes=64)
-            for j0 in range(lo, hi, P):
-                zt = psum.tile([P, NT, P], F32, name="zt", tag="zt", bufs=2)
-                for t in range(NT):
-                    nc.tensor.matmul(zt[:, t, :], te[t][:, j0 : j0 + P], ident[:], start=True, stop=False, is_transpose=True)
-                    nc.tensor.matmul(zt[:, t, :], tc3[t][:, j0 : j0 + P], ident[:], start=False, stop=True, is_transpose=True)
-                ztb = work.tile([P, 2, P, 2], BF16, name="ztb", tag="ztb", bufs=2)
-                nc.scalar.copy(ztb[:], zt[:].rearrange("j (u e) p -> j u p e", e=2))
-                words = ztb[:].rearrange("j u p e -> j (u p e)").bitcast(F32)
-                zw = psum.tile([P, 2, P], F32, name="zw", tag="zw", bufs=2)
+        def second_terms(b):
+            cols = slice(b * P, (b + 1) * P)
+            entries = l_n3[:, b * P // STRIPE : (b + 1) * P // STRIPE]
+            for t in range(TILES):
+                nc.vector.tensor_tensor(term2[t][:, cols], gained_d[t][:].indirect(entries), diff2[t][:, cols], ALU.mult)
+                last_in_bank = t == TILES - 1 or (t == 1 and b == BLOCKS - 1)
+                add_turned(term2[t], t, b, False, last_in_bank)
+
+        def turn_back(b):
+            z_rounded[b] = work.tile([P, P, 2], F32, name="z_rounded%d" % b, tag="z_rounded%d" % b, align_bytes=64)
+            back = bank("words%d" % (b % 2), HALF)
+            if b < BLOCKS - 1:
+                both = work.tile([P, 2, P, 2], BF16, name="both", tag="both", bufs=2)
+                nc.scalar.activation(both[:], turned[b][:].rearrange("j (u e p) -> j u p e", u=2, e=2), ACT.Copy, scale=0.5)
                 for u in range(2):
-                    nc.tensor.transpose(zw[:, u, :], words[:, u * P : (u + 1) * P], ident[:])
-                nc.scalar.copy(zb[lo][:, j0 - lo : j0 - lo + P, :], zw[:].rearrange("p u j -> p j u"))
+                    pairs = both[:, u, :, :].rearrange("j p e -> j (p e)").bitcast(F32)
+                    nc.tensor.transpose(back[:, u * P : (u + 1) * P], pairs, ident[:])
+            else:
+                for u in range(2):
+                    one = work.tile([P, P, 2], BF16, name="one", tag="one", bufs=2)
+                    nc.scalar.activation(one[:], turned_pairs[b][u].rearrange("j (e p) -> j p e", e=2), ACT.Copy, scale=0.5)
+                    pairs = one[:].rearrange("j p e -> j (p e)").bitcast(F32)
+                    nc.tensor.transpose(back[:, u * P : (u + 1) * P], pairs, ident[:])
+            nc.scalar.copy(z_rounded[b][:], back[:].rearrange("p (u j) -> p j u", u=2))
 
-        def quant_z(lo, hi):
-            nc.vector.quantize_mx(zq[:, lo:hi].bitcast(FP8X4), zs[:, lo:hi], zb[lo][:].rearrange("p j u -> p (j u)").bitcast(BF16))
+        def quantise_z(b):
+            cols = slice(b * P, (b + 1) * P)
+            values = z_rounded[b][:].rearrange("p j u -> p (j u)").bitcast(BF16)
+            nc.vector.quantize_mx(z_words[:, cols].bitcast(FP8X4), z_scales[:, cols], values)
 
-        first_terms(0, 256)
-        second_terms(0, 256)
-        turn(0, 256)
-        first_terms(256, 512)
-        second_terms(256, 384)
-        turn(256, 384)
-        quant_z(0, 256)
-        second_terms(384, 512)
-        turn(384, 512)
-        g_cand = gather_words(l_cand, "g_cand", "db", NT)
-        quant_z(256, 384)
-        g_candd = work.tile([P, S], U32, name="g_candd", align_bytes=64)
-        nc.vector.tensor_copy(
-            g_candd[:].rearrange("p (t c i) -> p c t i", t=NT, i=4),
-            g_cand[:].rearrange("p (c i t) -> p c t i", t=NT, i=4),
-        )
-        quant_z(384, 512)
+        first_terms()
+        for b in range(BLOCKS - 1):
+            second_terms(b)
+            turn_back(b)
+        quantise_z(0)
+        second_terms(BLOCKS - 1)
+        turn_back(BLOCKS - 1)
 
-        exp_plain = [work.tile([P, S], F32, name="exp%d" % t) for t in range(NT)]
-        e5 = [work.tile([P, S], F32, name="e5_%d" % t) for t in range(NT)]
-        num = [work.tile([P, S], F32, name="num%d" % t) for t in range(NT)]
-        den = [work.tile([P, S], F32, name="den%d" % t) for t in range(NT)]
-        accs = [product(g_candd, s_candd, t * P, zq, zs) for t in range(NT)]
+        words_cand = work.tile([P, S], U32, name="words_cand", tag="diff2", bufs=TILES, align_bytes=64)
+        gather_words(words_cand, l_cand, 0, S)
+
+        def deal_words(u, tag):
+            dealt = work.tile([P, 2 * P], U32, name="dealt_words%d" % u, tag=tag, align_bytes=64)
+            nc.vector.tensor_copy(
+                dealt[:].rearrange("p (e c i) -> p c e i", e=2, i=4),
+                words_cand[:].rearrange("p (c i t) -> p c t i", t=TILES, i=4)[:, :, 2 * u : 2 * u + 2, :],
+            )
+            return dealt
+
+        def deal_scales(u, tag):
+            dealt = work.tile([P, 2 * P], U8, name="dealt_scales%d" % u, tag=tag, align_bytes=64)
+            nc.vector.tensor_copy(
+                dealt[:].rearrange("p (e m) -> p e m", e=2),
+                scales_cand[:].rearrange("p (m t) -> p t m", t=TILES)[:, 2 * u : 2 * u + 2, :],
+            )
+            return dealt
+
+        dealt_words = [deal_words(0, "dealt_words0")]
+        dealt_scales = [deal_scales(0, "dealt_scales0")]
+        for b in range(1, BLOCKS):
+            quantise_z(b)
+        dealt_words.append(deal_words(1, "z_rounded3"))
+        dealt_scales.append(deal_scales(1, "z_rounded2"))
+        x_cand = [
+            (dealt_words[t // 2][:, (t % 2) * P : (t % 2 + 1) * P], dealt_scales[t // 2][:, (t % 2) * P : (t % 2 + 1) * P])
+            for t in range(TILES)
+        ]
+        z_mx = (z_words, z_scales)
+
+        ex_plain = [work.tile([P, S], F32, name="ex_plain%d" % t) for t in range(TILES)]
+        ex5 = [work.tile([P, S], F32, name="ex5_%d" % t) for t in range(TILES)]
+        num = [work.tile([P, S], F32, name="num%d" % t) for t in range(TILES)]
+        den = [work.tile([P, S], F32, name="den%d" % t) for t in range(TILES)]
+        early = bank("side0", LAST)
+        for lo in range(0, LAST, P):
+            mx_pass(early[:, lo : lo + P], x_cand[0], z_mx, lo, lo + P)
+        sums = {0: [(0, LAST, early), (LAST, S, product(x_cand[0], z_mx, "ring", LAST, S))]}
+        for t in range(1, TILES):
+            sums[t] = [(0, S, product(x_cand[t], z_mx, "ring"))]
 
         def ex_tile(t):
-            nc.scalar.activation(win[t][:, :S], accs[t][:], ACT.Exp, scale=0.03125)
-            nc.sync.dma_start(exp_plain[t][:], win[t][:, :S])
+            for lo, hi, acc in sums[t]:
+                nc.scalar.activation(rows[t][:, lo:hi], acc[:], ACT.Exp, scale=EXP_SCALE)
+            nc.sync.dma_start(ex_plain[t][:], rows[t][:, :S])
 
-        def u_tile(t):
-            nc.scalar.activation(uwin[t][:, :S], accs[t][:], ACT.Copy, scale=0.03125)
+        def arg_tile(t):
+            nc.scalar.activation(args[t][:, :S], sums[t][0][2][:], ACT.Copy, scale=EXP_SCALE)
 
-        def e5_tile(t):
-            nc.scalar.activation(e5[t][:], uwin[t][:].indirect(l_n5[:]), ACT.Exp)
+        def ex5_on_scalar(t):
+            nc.scalar.activation(ex5[t][:], args[t][:].indirect(l_n5[:]), ACT.Exp)
 
         ex_tile(0)
-        nc.vector.tensor_copy(e5[0][:], win[0][:].indirect(l_n5[:]))
-        u_tile(1)
+        nc.vector.tensor_copy(ex5[0][:], rows[0][:].indirect(l_n5[:]))
+        arg_tile(1)
         ex_tile(1)
-        e5_tile(1)
-        u_tile(2)
+        ex5_on_scalar(1)
+        arg_tile(2)
         ex_tile(2)
-        u_tile(3)
-        e5_tile(2)
+        arg_tile(3)
+        ex5_on_scalar(2)
         ex_tile(3)
-        e5_tile(3)
-        for t in range(NT):
-            nc.vector.tensor_tensor(den[t][:], win[t][:].indirect(l_n6[:]), e5[t][:], ALU.add)
-            nc.vector.tensor_tensor(num[t][:], win[t][:].indirect(l_n4[:]), exp_plain[t][:], ALU.add)
-        out_rows = out.rearrange("(p t) n -> p t n", t=NT)
-        logs = work.tile([P, 2 * NT * S], F32, name="logs", tag="uwin3")
-        for t in range(NT):
-            lden = logs[:, 2 * t * S : (2 * t + 1) * S]
-            lnum = logs[:, (2 * t + 1) * S : (2 * t + 2) * S]
-            nc.scalar.activation(lden, den[t][:], ACT.Ln)
-            nc.scalar.activation(lnum, num[t][:], ACT.Ln)
-            res = work.tile([P, S], F32, name="res%d" % t)
-            nc.vector.tensor_tensor(res[:], lnum, lden, ALU.subtract)
-            nc.sync.dma_start(out_rows[:, t, :], res[:])
+        ex5_on_scalar(3)
+        for t in range(TILES):
+            nc.vector.tensor_tensor(den[t][:], rows[t][:].indirect(l_n6[:]), ex5[t][:], ALU.add)
+            nc.vector.tensor_tensor(num[t][:], rows[t][:].indirect(l_n4[:]), ex_plain[t][:], ALU.add)
+
+        out_rows = out.rearrange("(p t) n -> p t n", t=TILES)
+        logs = work.tile([P, 2 * TILES * S], F32, name="logs", tag="args3")
+        for t in range(TILES):
+            ln_den = logs[:, 2 * t * S : (2 * t + 1) * S]
+            ln_num = logs[:, (2 * t + 1) * S : (2 * t + 2) * S]
+            nc.scalar.activation(ln_den, den[t][:], ACT.Ln)
+            for lo, hi in ((0, HALF), (HALF, S)) if t == TILES - 1 else ((0, S),):
+                nc.scalar.activation(ln_num[:, lo:hi], num[t][:, lo:hi], ACT.Ln)
+                result = work.tile([P, hi - lo], F32, name="result%d_%d" % (t, lo))
+                nc.vector.tensor_tensor(result[:], ln_num[:, lo:hi], ln_den[:, lo:hi], ALU.subtract)
+                nc.sync.dma_start(out_rows[:, t, lo:hi], result[:])

from contextlib import ExitStack

import concourse.mybir as mybir
from concourse.masks import make_identity

FLOPS = 3 * 2 * 512 * 512 * 512

F32 = mybir.dt.float32
BF16 = mybir.dt.bfloat16
I32 = mybir.dt.int32
U32 = mybir.dt.uint32
U16 = mybir.dt.uint16
U8 = mybir.dt.uint8
FP8X4 = mybir.dt.float8_e4m3fn_x4
ALU = mybir.AluOpType
ACT = mybir.ActivationFunctionType

P = 128
T = 2048
S = 512
HALF = S // 2
TILES = 4
BLOCKS = S // P
LAST = S - P
STRIPE = 16
EXP_SCALE = 0.5 * 0.0625
SCALAR_TILES = (1, 2, 3)


def tile_picked_twcflowbodds_none_p_kernel(
    tc, x_words, x_scales, w1, w2, gs, offs, two, n1, n2, n3, cand, n4, n5, n6, out
):
    nc = tc.nc
    with ExitStack() as ctx:
        lists = ctx.enter_context(tc.tile_pool(name="lists", bufs=1))
        work = ctx.enter_context(tc.tile_pool(name="work", bufs=1))
        psum = ctx.enter_context(tc.psum_pool(name="psum", bufs=1))

        def load_list(src, name):
            offsets = lists.tile([P, S // STRIPE], U16, name=name)
            nc.sync.dma_start(offsets[:], src)
            return offsets

        scale_table = work.tile([P, T], U8, name="scale_table")
        nc.gpsimd.memset(scale_table[:].bitcast(I32), 0)
        l_offs = load_list(offs, "l_offs")
        l_two = load_list(two, "l_two")
        w1_raw = work.tile([P, TILES, S], F32, name="w1_raw")
        w1_rows = w1.rearrange("(p j) c -> p j c", j=TILES)
        nc.sync.dma_start(w1_raw[:, 0, :], w1_rows[:, 0, :])
        for quad in range(4):
            nc.sync.dma_start(
                scale_table[32 * quad : 32 * quad + 4, :].bitcast(I32),
                x_scales[0, 4 * quad : 4 * quad + 4, :].bitcast(I32),
            )
        nc.sync.dma_start(w1_raw[:, 1:, :], w1_rows[:, 1:, :])
        l_cand = load_list(cand, "l_cand")
        word_table = work.tile([P, T], I32, name="word_table")
        nc.sync.dma_start(word_table[:], x_words[0].rearrange("p n t -> p (n t)").bitcast(I32))
        l_n1 = load_list(n1, "l_n1")
        l_n2 = load_list(n2, "l_n2")
        w2_raw = work.tile([P, TILES, S], F32, name="w2_raw")
        nc.sync.dma_start(w2_raw[:], w2.rearrange("(p j) c -> p j c", j=TILES))
        gains = work.tile([P, TILES], F32, name="gains")
        nc.sync.dma_start(gains[:], gs.rearrange("(p t) o -> p (t o)", t=TILES))
        l_n3 = load_list(n3, "l_n3")
        l_n5 = load_list(n5, "l_n5")
        l_n6 = load_list(n6, "l_n6")
        l_n4 = load_list(n4, "l_n4")

        rows = [work.tile([P, 2 * S], F32, name="rows%d" % t) for t in range(TILES)]
        nc.vector.memset(rows[0][:, S : S + HALF], 0.0)
        nc.scalar.copy(rows[0][:, S + HALF :], rows[0][:, S : S + HALF])
        ident = work.tile([P, P], F32, name="ident")
        make_identity(nc, ident[:])
        args = {t: work.tile([P, 2 * S], F32, name="args%d" % t, tag="args%d" % t) for t in SCALAR_TILES}

        def gather_scales(offsets, name):
            picked = work.tile([P, S], U8, name=name, align_bytes=64)
            nc.vector.tensor_copy(picked[:], scale_table[:].indirect(offsets[:]))
            return picked

        def gather_words(picked, offsets, lo, hi):
            entries = offsets[:, lo // STRIPE : hi // STRIPE]
            nc.vector.tensor_copy(picked[:, lo:hi], word_table[:].bitcast(U32).indirect(entries))

        def cast_pair(raw, u, name):
            rounded = work.tile([P, 2, P, TILES], BF16, name=name, align_bytes=64)
            nc.scalar.copy(
                rounded[:].rearrange("p e m j -> p m j e"),
                raw[:].rearrange("p j (m t) -> p m j t", t=TILES)[:, :, :, 2 * u : 2 * u + 2],
            )
            return rounded

        def quantise_weights(rounded, e0, e1, name, tag):
            words = work.tile([P, (e1 - e0) * P], U32, name=name + "_words", tag=tag, align_bytes=64)
            scales = work.tile([P, (e1 - e0) * P], U8, name=name + "_scales", align_bytes=64)
            values = rounded[:, e0:e1, :, :].rearrange("p e m j -> p (e m j)")
            nc.vector.quantize_mx(words[:].bitcast(FP8X4), scales[:], values)
            return [(words[:, e * P : (e + 1) * P], scales[:, e * P : (e + 1) * P]) for e in range(e1 - e0)]

        def bank(tag, width):
            return psum.tile([P, width], F32, name=tag, tag=tag, bufs=TILES if tag == "ring" else 1)

        def mx_pass(dst, stationary, moving, lo, hi):
            nc.tensor.matmul_mx(
                dst,
                lhsT=stationary[0].bitcast(FP8X4),
                lhsT_scale=stationary[1],
                rhs=moving[0][:, lo:hi].bitcast(FP8X4),
                rhs_scale=moving[1][:, lo:hi],
                start=True,
                stop=True,
            )

        def product(stationary, moving, tag, lo=0, hi=S):
            acc = bank(tag, hi - lo)
            mx_pass(acc[:], stationary, moving, lo, hi)
            return acc

        scales_offs = gather_scales(l_offs, "scales_offs")
        scales_two = gather_scales(l_two, "scales_two")
        w1_rounded = [cast_pair(w1_raw, u, "w1_rounded%d" % u) for u in range(2)]
        w1q = quantise_weights(w1_rounded[0], 0, 1, "w1q0", "w1q0")
        w1q = w1q + quantise_weights(w1_rounded[0], 1, 2, "w1q1", "w1q1")
        scales_cand = gather_scales(l_cand, "scales_cand")
        words_offs = work.tile([P, S], U32, name="words_offs", align_bytes=64)
        for lo in (0, HALF):
            gather_words(words_offs, l_offs, lo, lo + HALF)
        words_two = work.tile([P, S], U32, name="words_two", align_bytes=64)
        gather_words(words_two, l_two, 0, S)
        x_offs = (words_offs, scales_offs)
        x_two = (words_two, scales_two)

        y_plain = [rows[t + 1][:, S:] for t in range(TILES - 1)] + [work.tile([P, S], F32, name="y_plain3")[:]]
        diff1 = [args[t][:, S:] if t in args else work.tile([P, S], F32, name="diff1_%d" % t)[:] for t in range(TILES)]
        diff2 = [
            work.tile([P, S], F32, name="diff2_%d" % t, tag="diff2", bufs=TILES, align_bytes=64) for t in range(TILES)
        ]
        gained_d = [work.tile([P, S], F32, name="gained_d%d" % t) for t in range(TILES)]
        w2q = []

        def y_tile(t):
            for lo, hi in ((0, HALF), (HALF, S)) if t == 0 else ((0, S),):
                acc = product(w1q[t], x_offs, "ring", lo, hi)
                nc.scalar.copy(rows[t][:, lo:hi], acc[:])
                nc.scalar.copy(y_plain[t][:, lo:hi], acc[:])

        def differences(t):
            nc.vector.tensor_tensor(diff1[t], rows[t][:].indirect(l_n1[:]), y_plain[t], ALU.subtract)
            nc.vector.tensor_tensor(diff2[t][:], rows[t][:].indirect(l_n2[:]), y_plain[t], ALU.subtract)

        def d_tile(t):
            acc = product(w2q[t], x_two, "side%d" % (t % 2))
            nc.scalar.activation(gained_d[t][:], acc[:], ACT.Copy, scale=gains[:, t : t + 1])

        y_tile(0)
        w1q.extend(quantise_weights(w1_rounded[1], 0, 2, "w1q2", "w1q0"))
        y_tile(1)
        differences(0)
        w2_rounded0 = cast_pair(w2_raw, 0, "w2_rounded0")
        y_tile(2)
        differences(1)
        w2q.extend(quantise_weights(w2_rounded0, 0, 2, "w2q0", "w2q0"))
        w2_rounded1 = cast_pair(w2_raw, 1, "w2_rounded1")
        y_tile(3)
        differences(2)
        w2q.extend(quantise_weights(w2_rounded1, 0, 2, "w2q2", "w2q2"))
        for t in range(TILES):
            d_tile(t)
        differences(3)

        term1 = [work.tile([P, S], F32, name="term1_%d" % t) for t in range(TILES)]
        term2 = [work.tile([P, S], F32, name="term2_%d" % t) for t in range(TILES)]
        z_words = work.tile([P, S], U32, name="z_words", align_bytes=64)
        z_scales = work.tile([P, S], U8, name="z_scales", align_bytes=64)
        turned = [bank("ring", S) for b in range(BLOCKS)]
        turned_pairs = [[turned[b][:, :HALF], turned[b][:, HALF:]] for b in range(BLOCKS - 1)]
        turned_pairs.append([turned[BLOCKS - 1][:, :HALF], bank("side0", HALF)[:]])
        z_rounded = {}

        def add_turned(term, t, b, start, stop):
            dst = turned_pairs[b][t // 2][:, (t % 2) * P : (t % 2 + 1) * P]
            nc.tensor.matmul(dst, term[:, b * P : (b + 1) * P], ident[:], start=start, stop=stop, is_transpose=True)

        def first_terms():
            for t in range(TILES):
                nc.vector.scalar_tensor_tensor(term1[t][:], gained_d[t][:], 2.0, diff1[t], ALU.mult, ALU.mult)
                for b in range(BLOCKS):
                    first_in_bank = t == 0 or (t == 2 and b == BLOCKS - 1)
                    add_turned(term1[t], t, b, first_in_bank, False)

        def second_terms(b):
            cols = slice(b * P, (b + 1) * P)
            entries = l_n3[:, b * P // STRIPE : (b + 1) * P // STRIPE]
            for t in range(TILES):
                nc.vector.tensor_tensor(term2[t][:, cols], gained_d[t][:].indirect(entries), diff2[t][:, cols], ALU.mult)
                last_in_bank = t == TILES - 1 or (t == 1 and b == BLOCKS - 1)
                add_turned(term2[t], t, b, False, last_in_bank)

        def turn_back(b):
            z_rounded[b] = work.tile([P, P, 2], F32, name="z_rounded%d" % b, tag="z_rounded%d" % b, align_bytes=64)
            back = bank("words%d" % (b % 2), HALF)
            if b < BLOCKS - 1:
                both = work.tile([P, 2, P, 2], BF16, name="both", tag="both", bufs=2)
                nc.scalar.activation(both[:], turned[b][:].rearrange("j (u e p) -> j u p e", u=2, e=2), ACT.Copy, scale=0.5)
                for u in range(2):
                    pairs = both[:, u, :, :].rearrange("j p e -> j (p e)").bitcast(F32)
                    nc.tensor.transpose(back[:, u * P : (u + 1) * P], pairs, ident[:])
            else:
                for u in range(2):
                    one = work.tile([P, P, 2], BF16, name="one", tag="one", bufs=2)
                    nc.scalar.activation(one[:], turned_pairs[b][u].rearrange("j (e p) -> j p e", e=2), ACT.Copy, scale=0.5)
                    pairs = one[:].rearrange("j p e -> j (p e)").bitcast(F32)
                    nc.tensor.transpose(back[:, u * P : (u + 1) * P], pairs, ident[:])
            nc.scalar.copy(z_rounded[b][:], back[:].rearrange("p (u j) -> p j u", u=2))

        def quantise_z(b):
            cols = slice(b * P, (b + 1) * P)
            values = z_rounded[b][:].rearrange("p j u -> p (j u)").bitcast(BF16)
            nc.vector.quantize_mx(z_words[:, cols].bitcast(FP8X4), z_scales[:, cols], values)

        first_terms()
        for b in range(BLOCKS - 1):
            second_terms(b)
            turn_back(b)
        quantise_z(0)
        second_terms(BLOCKS - 1)
        turn_back(BLOCKS - 1)

        words_cand = work.tile([P, S], U32, name="words_cand", tag="diff2", bufs=TILES, align_bytes=64)
        gather_words(words_cand, l_cand, 0, S)

        def deal_words(u, tag):
            dealt = work.tile([P, 2 * P], U32, name="dealt_words%d" % u, tag=tag, align_bytes=64)
            nc.vector.tensor_copy(
                dealt[:].rearrange("p (e c i) -> p c e i", e=2, i=4),
                words_cand[:].rearrange("p (c i t) -> p c t i", t=TILES, i=4)[:, :, 2 * u : 2 * u + 2, :],
            )
            return dealt

        def deal_scales(u, tag):
            dealt = work.tile([P, 2 * P], U8, name="dealt_scales%d" % u, tag=tag, align_bytes=64)
            nc.vector.tensor_copy(
                dealt[:].rearrange("p (e m) -> p e m", e=2),
                scales_cand[:].rearrange("p (m t) -> p t m", t=TILES)[:, 2 * u : 2 * u + 2, :],
            )
            return dealt

        dealt_words = [deal_words(0, "dealt_words0")]
        dealt_scales = [deal_scales(0, "dealt_scales0")]
        for b in range(1, BLOCKS):
            quantise_z(b)
        dealt_words.append(deal_words(1, "z_rounded3"))
        dealt_scales.append(deal_scales(1, "z_rounded2"))
        x_cand = [
            (dealt_words[t // 2][:, (t % 2) * P : (t % 2 + 1) * P], dealt_scales[t // 2][:, (t % 2) * P : (t % 2 + 1) * P])
            for t in range(TILES)
        ]
        z_mx = (z_words, z_scales)

        ex_plain = [work.tile([P, S], F32, name="ex_plain%d" % t) for t in range(TILES)]
        ex5 = [work.tile([P, S], F32, name="ex5_%d" % t) for t in range(TILES)]
        num = [work.tile([P, S], F32, name="num%d" % t) for t in range(TILES)]
        den = [work.tile([P, S], F32, name="den%d" % t) for t in range(TILES)]
        early = bank("side0", LAST)
        for lo in range(0, LAST, P):
            mx_pass(early[:, lo : lo + P], x_cand[0], z_mx, lo, lo + P)
        sums = {0: [(0, LAST, early), (LAST, S, product(x_cand[0], z_mx, "ring", LAST, S))]}
        for t in range(1, TILES):
            sums[t] = [(0, S, product(x_cand[t], z_mx, "ring"))]

        def ex_tile(t):
            for lo, hi, acc in sums[t]:
                nc.scalar.activation(rows[t][:, lo:hi], acc[:], ACT.Exp, scale=EXP_SCALE)
            nc.sync.dma_start(ex_plain[t][:], rows[t][:, :S])

        def arg_tile(t):
            nc.scalar.activation(args[t][:, :S], sums[t][0][2][:], ACT.Copy, scale=EXP_SCALE)

        def ex5_on_scalar(t):
            nc.scalar.activation(ex5[t][:], args[t][:].indirect(l_n5[:]), ACT.Exp)

        ex_tile(0)
        nc.vector.tensor_copy(ex5[0][:], rows[0][:].indirect(l_n5[:]))
        arg_tile(1)
        ex_tile(1)
        ex5_on_scalar(1)
        arg_tile(2)
        ex_tile(2)
        arg_tile(3)
        ex5_on_scalar(2)
        ex_tile(3)
        ex5_on_scalar(3)
        for t in range(TILES):
            nc.vector.tensor_tensor(den[t][:], rows[t][:].indirect(l_n6[:]), ex5[t][:], ALU.add)
            nc.vector.tensor_tensor(num[t][:], rows[t][:].indirect(l_n4[:]), ex_plain[t][:], ALU.add)

        out_rows = out.rearrange("(p t) n -> p t n", t=TILES)
        logs = work.tile([P, 2 * TILES * S], F32, name="logs", tag="args3")
        for t in range(TILES):
            ln_den = logs[:, 2 * t * S : (2 * t + 1) * S]
            ln_num = logs[:, (2 * t + 1) * S : (2 * t + 2) * S]
            nc.scalar.activation(ln_den, den[t][:], ACT.Ln)
            for lo, hi in ((0, HALF), (HALF, S)) if t == TILES - 1 else ((0, S),):
                nc.scalar.activation(ln_num[:, lo:hi], num[t][:, lo:hi], ACT.Ln)
                result = work.tile([P, hi - lo], F32, name="result%d_%d" % (t, lo))
                nc.vector.tensor_tensor(result[:], ln_num[:, lo:hi], ln_den[:, lo:hi], ALU.subtract)
                nc.sync.dma_start(out_rows[:, t, lo:hi], result[:])
